import numpy as np
import ml_dtypes


def mxq(x, axis, fmt="e4m3"):
    dtype, down = {"e4m3": (ml_dtypes.float8_e4m3fn, 7), "e5m2": (ml_dtypes.float8_e5m2, 14)}[fmt]
    v = np.moveaxis(np.asarray(x, np.float32).astype(ml_dtypes.bfloat16).astype(np.float64), axis, -1)
    blocks = v.reshape(v.shape[:-1] + (-1, 32))
    amax = np.abs(blocks).max(-1, keepdims=True)
    byte = np.maximum(np.where(amax > 0, np.frexp(amax)[1] - 1 + 127, 0) - down, 1)
    scale = np.exp2(byte - 127.0)
    codes = (blocks / scale).astype(np.float32).astype(dtype).astype(np.float64)
    return np.moveaxis((codes * scale).reshape(v.shape), -1, axis)


WIDE = False


def mx_kscale(k):
    if not WIDE:
        return np.ones(k)
    levels = np.array([10, -10, 5, -5, 0])
    if k % 512:
        return np.exp2(np.random.permutation(np.resize(levels, k // 32))).repeat(32)
    a = np.empty((k // 512, 16))
    for p in range(k // 512):
        a[p, :8] = np.random.permutation(np.resize(levels, 8))
        for g in range(8):
            far = levels[np.abs(levels - a[p, g]) >= 10]
            a[p, g + 8] = far[np.random.randint(len(far))]
    return np.exp2(a.ravel()).repeat(32)


def f64(x):
    return np.asarray(x).astype(np.float64)


def striped(idx):
    return np.tile(np.asarray(idx).reshape(-1, 16).T, (8, 1)).astype(np.uint16)


def unstriped(offs):
    return offs[:16].T.reshape(-1).astype(np.int64)


E2M1 = np.array([0.0, 0.5, 1.0, 1.5, 2.0, 3.0, 4.0, 6.0, -0.0, -0.5, -1.0, -1.5, -2.0, -3.0, -4.0, -6.0])


def pack_weight(w, fmt):
    k, n = w.shape
    w = f64(np.asarray(w, np.float32).astype(ml_dtypes.bfloat16)).reshape(k // 32, 32, n)
    amax = np.abs(w).max(1)
    if fmt == "e4m3":
        byte = np.frexp(amax)[1] - 1 + 127 - 7
    else:
        mant, ex = np.frexp(amax / 6.0)
        byte = np.where(mant > 0.5, ex, ex - 1) + 127
    byte = np.clip(np.where(amax > 0, byte, 1), 1, 254)
    scaled = (w * np.exp2(127.0 - byte)[:, None, :]).reshape(k, n).astype(np.float32)
    by_word = np.ascontiguousarray(scaled.reshape(k // 512, 128, 4, n).transpose(0, 1, 3, 2))
    if fmt == "e4m3":
        words = by_word.astype(ml_dtypes.float8_e4m3fn).view(np.uint8)
    else:
        c = by_word.astype(ml_dtypes.float4_e2m1fn).view(np.uint8) & 0xF
        words = (c[..., 0::2] | (c[..., 1::2] << 4)).reshape(k // 512, 128, 2 * n)
    return np.ascontiguousarray(words), np.ascontiguousarray(byte.astype(np.uint8).reshape(k // 512, 16, n))


def unpack_weight(words, scales, fmt):
    g, _, n = scales.shape
    words = np.ascontiguousarray(words).reshape(g, 128, n, -1)
    if fmt == "e4m3":
        vals = words.view(ml_dtypes.float8_e4m3fn).astype(np.float64)
    else:
        nib = np.empty((g, 128, n, 4), np.uint8)
        nib[..., 0::2] = words & 0xF
        nib[..., 1::2] = words >> 4
        vals = E2M1[nib]
    vals = vals * np.repeat(np.exp2(scales.astype(np.float64) - 127.0), 8, axis=1)[..., None]
    return vals.transpose(0, 1, 3, 2).reshape(g * 512, n)


def softplus(v):
    return np.log(1.0 + np.exp(v))


D, K, R, T, I, Q = 512, 512, 512, 2048, 512, 128


def setup_inputs():
    n = np.random.standard_normal
    idx3 = np.random.permutation(I)[:I]
    idx = np.random.permutation(T)[:I]
    fd = mx_kscale(D)
    fk = mx_kscale(K)
    fi = mx_kscale(I)
    keysp = pack_weight(n((D, T)) / fd[:, None], "e4m3")
    tabp = pack_weight(n((K, T)) / fk[:, None], "e4m3")
    return {
        "query": (n((D, Q)) * 0.7 / np.sqrt(D) * fd[:, None]).astype(np.float32),
        "keys_words": keysp[0],
        "keys_scales": keysp[1],
        "tab_words": tabp[0],
        "tab_scales": tabp[1],
        "w1": (n((K, R)) * 1 / np.sqrt(K) * fk[:, None]).astype(np.float32),
        "lam": (np.random.uniform(0.3, 1.0, (R, 1))).astype(np.float32),
        "os": (np.random.uniform(4.0, 16.0, (1, I)) * fi).astype(np.float32),
        "vs": (np.random.uniform(0.5, 2.0, (1, I)) / fi).astype(np.float32),
        "offs3": striped(idx3),
        "offs": striped(idx),
    }


def reference(query, keys_words, keys_scales, tab_words, tab_scales, w1, lam, os, vs, offs3, offs):
    idx3 = unstriped(offs3)
    idx = unstriped(offs)
    keysu = unpack_weight(keys_words, keys_scales, "e4m3")
    tabu = unpack_weight(tab_words, tab_scales, "e4m3")
    queryq = mxq(f64(query), 0, "e4m3")
    keysidxg = keysu[:, idx]
    a = queryq.T @ keysidxg
    p = np.exp(a - np.max(a, axis=1, keepdims=True))
    z = np.sum(p, axis=1, keepdims=True)
    w = p / z
    w1q = mxq(f64(w1), 0, "e4m3")
    tabidxg = tabu[:, idx]
    zh = w1q.T @ tabidxg
    ht = softplus(zh)
    hv = ht + ht[:, idx3] * f64(lam)
    wo1 = w * f64(os)
    wt1 = wo1.T
    hw = hv * f64(vs)
    ht1 = hw.T
    wt1q = mxq(wt1, 0, "e4m3")
    ht1q = mxq(ht1, 0, "e4m3")
    o = wt1q.T @ ht1q
    return o

@@ -1,0 +1,221 @@
+from contextlib import ExitStack
+
+import concourse.mybir as mybir
+from concourse.masks import make_identity
+
+F32 = mybir.dt.float32
+BF16 = mybir.dt.bfloat16
+I32 = mybir.dt.int32
+U32 = mybir.dt.uint32
+U16 = mybir.dt.uint16
+U8 = mybir.dt.uint8
+FP8X4 = mybir.dt.float8_e4m3fn_x4
+ACT = mybir.ActivationFunctionType
+ALU = mybir.AluOpType
+AX = mybir.AxisListType
+
+P = 128
+PACK = 4
+POOL = 2048
+SLOTS = 512
+HIDDEN = 512
+ROWS = 128
+TILES = HIDDEN // P
+LINEAR_FROM = 40.0
+
+FLOPS = 2 * 512 * ROWS * SLOTS + 2 * 512 * HIDDEN * SLOTS + 2 * SLOTS * ROWS * HIDDEN
+
+
+def tile_attend_lrlent_soft_kernel(tc, query, keys_words, keys_scales, tab_words, tab_scales, w1, lam,
+                                    slot_factor, value_scale, offs3, offs, out):
+    nc = tc.nc
+    with ExitStack() as ctx:
+        keep = ctx.enter_context(tc.tile_pool(name="keep", bufs=1))
+        shared = ctx.enter_context(tc.tile_pool(name="shared", bufs=1))
+        psum = ctx.enter_context(tc.psum_pool(name="psum", bufs=1))
+
+        def load_scales(name, scales):
+            plane = keep.tile([P, POOL], U8, name=name, align_bytes=64)
+            nc.gpsimd.memset(plane[:].bitcast(I32), 0)
+            for quad in range(4):
+                nc.sync.dma_start(out=plane[32 * quad:32 * quad + 4, :].bitcast(I32),
+                                  in_=scales[0, 4 * quad:4 * quad + 4, :].bitcast(I32))
+            return plane
+
+        def load_scales_repeated(name, scales):
+            plane = keep.tile([P, POOL], U8, name=name, align_bytes=64)
+            for quad in range(4):
+                rows = scales[0, 4 * quad:4 * quad + 4, :].bitcast(I32)
+                nc.sync.dma_start(out=plane[32 * quad:32 * quad + 32, :].bitcast(I32),
+                                  in_=rows.unsqueeze(0).to_broadcast([8, 4, POOL // 4]))
+            return plane
+
+        def load_words(pool_words, words):
+            nc.sync.dma_start(out=pool_words[:], in_=words[0].rearrange("p n t -> p (n t)").bitcast(I32))
+            return pool_words
+
+        def gather_scales(name, plane, tag):
+            picked = keep.tile([P, SLOTS], U8, name=name, tag=tag, align_bytes=64)
+            nc.vector.tensor_copy(out=picked[:], in_=plane[:].indirect(tokens[:]))
+            return picked
+
+        def gather_words(name, pool_words):
+            picked = keep.tile([P, SLOTS], U32, name=name, align_bytes=64)
+            nc.vector.tensor_copy(out=picked[:], in_=pool_words[:].bitcast(U32).indirect(tokens[:]))
+            return picked
+
+        def quantize(name, grouped):
+            codes = keep.tile([P, P], U32, name=name + "_codes", align_bytes=64)
+            scales = keep.tile([P, P], U8, name=name + "_scales", align_bytes=64)
+            nc.vector.quantize_mx(out=codes[:].bitcast(FP8X4), scales=scales[:],
+                                  in_=grouped[:].rearrange("p c t -> p (c t)"))
+            return codes, scales
+
+        def weave(name, raw, on_scalar, tag):
+            grouped = keep.tile([P, P, PACK], BF16, name=name, tag=tag, align_bytes=64)
+            dst = grouped[:].rearrange("p (c i) t -> p c t i", i=4)
+            src = raw.rearrange("p t (c i) -> p c t i", i=4)
+            if on_scalar:
+                nc.scalar.activation(out=dst, in_=src, func=ACT.Copy)
+            else:
+                nc.vector.tensor_copy(out=dst, in_=src)
+            return grouped
+
+        tokens = keep.tile([P, SLOTS // 16], U16, name="tokens")
+        nc.sync.dma_start(tokens[:], offs)
+        tab_plane = load_scales_repeated("tab_plane", tab_scales)
+        tab_pool = load_words(keep.tile([P, POOL], I32, name="tab_pool", align_bytes=64), tab_words)
+        w1_rows = w1.rearrange("(p t) r -> p t r", t=PACK)
+        w1_raw = []
+        for half in range(2):
+            raw = keep.tile([P, PACK, 2 * P], F32, name="w1_raw%d" % half, align_bytes=64)
+            nc.sync.dma_start(out=raw[:], in_=w1_rows[:, :, 2 * P * half:2 * P * (half + 1)])
+            w1_raw.append(raw)
+        keys_plane = load_scales("keys_plane", keys_scales)
+        query_raw = keep.tile([P, PACK, ROWS], F32, name="query_raw", align_bytes=64)
+        nc.sync.dma_start(out=query_raw[:], in_=query.rearrange("(p t) q -> p t q", t=PACK))
+        keys_pool = load_words(shared.tile([P, POOL], I32, name="keys_pool", align_bytes=64, offset=0), keys_words)
+        links = keep.tile([P, SLOTS // 16], U16, name="links")
+        nc.sync.dma_start(links[:], offs3)
+        lam_col = keep.tile([P, TILES], F32, name="lam_col")
+        with nc.allow_non_contiguous_dma(reason="one factor a partition and tile"):
+            nc.sync.dma_start(out=lam_col[:], in_=lam.rearrange("(j p) o -> p (j o)", p=P))
+        vs_col = keep.tile([P, PACK], F32, name="vs_col")
+        nc.sync.dma_start(out=vs_col[:], in_=value_scale.rearrange("o (p t) -> p (o t)", t=PACK))
+        os_col = keep.tile([P, PACK], F32, name="os_col")
+        nc.sync.dma_start(out=os_col[:], in_=slot_factor.rearrange("o (p t) -> p (o t)", t=PACK))
+
+        ident = keep.tile([P, P], F32, name="ident", align_bytes=64)
+        make_identity(nc, ident[:])
+
+        tab_s = gather_scales("tab_s", tab_plane, "tab_s")
+        tab_w = gather_words("tab_w", tab_pool)
+        zh = []
+        grown = []
+        for j in range(TILES):
+            raw = w1_raw[j // 2][:, :, P * (j % 2):P * (j % 2 + 1)]
+            codes, scales = quantize("w1q%d" % j, weave("w1g%d" % j, raw, j == 1, "w1g%d" % j))
+            bank = psum.tile([P, SLOTS], F32, name="zh%d" % j, tag="zh%d" % j)
+            nc.tensor.matmul_mx(out=bank[:], lhsT=codes[:].bitcast(FP8X4), lhsT_scale=scales[:],
+                                rhs=tab_w[:].bitcast(FP8X4), rhs_scale=tab_s[:], start=True, stop=True)
+            e = keep.tile([P, SLOTS], F32, name="grown%d" % j)
+            nc.scalar.activation(out=e[:], in_=bank[:], func=ACT.Exp)
+            zh.append(bank)
+            grown.append(e)
+
+        keys_s = gather_scales("keys_s", keys_plane, "w1g3")
+        q_codes, q_scales = quantize("qq", weave("qg", query_raw[:], False, "w1g2"))
+        keys_w = gather_words("keys_w", keys_pool)
+        scores = psum.tile([P, SLOTS], F32, name="scores", tag="scores")
+        nc.tensor.matmul_mx(out=scores[:], lhsT=q_codes[:].bitcast(FP8X4), lhsT_scale=q_scales[:],
+                            rhs=keys_w[:].bitcast(FP8X4), rhs_scale=keys_s[:], start=True, stop=True)
+
+        logs = []
+        for j in range(TILES):
+            lg = keep.tile([P, SLOTS], F32, name="log%d" % j)
+            nc.scalar.activation(out=lg[:], in_=grown[j][:], func=ACT.Ln, bias=1.0)
+            logs.append(lg)
+
+        def softplus(j):
+            ht = shared.tile([P, SLOTS], F32, name="ht%d" % j, align_bytes=64, offset=4 * SLOTS * j)
+            nc.vector.scalar_tensor_tensor(out=ht[:], in0=logs[j][:], scalar=LINEAR_FROM, in1=zh[j][:],
+                                           op0=ALU.min, op1=ALU.max)
+            return ht
+
+        def look_up(j, half, on_scalar):
+            cols = slice(256 * half, 256 * (half + 1))
+            picked = hts[j][:].indirect(links[:, 16 * half:16 * (half + 1)])
+            if on_scalar:
+                nc.scalar.activation(out=linked[j][:, cols], in_=picked, func=ACT.Copy)
+            else:
+                nc.vector.tensor_copy(out=linked[j][:, cols], in_=picked)
+
+        def turn_own(j):
+            bank = psum.tile([P, PACK, P], F32, name="turned%d" % j, tag="zh%d" % j)
+            for t in range(PACK):
+                nc.tensor.matmul(bank[:, t, :], lhsT=hts[j][:, t:SLOTS:PACK], rhs=ident[:], start=(t == 0),
+                                 stop=False, is_transpose=True)
+            return bank
+
+        def add_linked(j, tag):
+            term = keep.tile([P, PACK, P], F32, name="term%d" % j, tag=tag, align_bytes=64)
+            nc.gpsimd.tensor_scalar(out=term[:], in0=linked[j][:].rearrange("p (s t) -> p t s", t=PACK),
+                                    scalar1=lam_col[:, j:j + 1], scalar2=0.0, op0=ALU.mult, op1=ALU.add)
+            for t in range(PACK):
+                nc.tensor.matmul(turned[j][:, t, :], lhsT=term[:, t, :], rhs=ident[:], start=False,
+                                 stop=(t == PACK - 1), is_transpose=True)
+
+        def scale_round(name, bank, col, tag):
+            grouped = keep.tile([P, P, PACK], BF16, name=name, tag=tag, align_bytes=64)
+            nc.vector.tensor_tensor(out=grouped[:], in0=bank[:].rearrange("p t c -> p c t"),
+                                    in1=col[:].unsqueeze(1).to_broadcast([P, P, PACK]), op=ALU.mult)
+            return grouped
+
+        def read_out(j, codes, scales):
+            acc = psum.tile([P, P], F32, name="acc%d" % j, tag="acc%d" % (j % 2))
+            nc.tensor.matmul_mx(out=acc[:], lhsT=w_codes[:].bitcast(FP8X4), lhsT_scale=w_scales[:],
+                                rhs=codes[:].bitcast(FP8X4), rhs_scale=scales[:], start=True, stop=True)
+            result = keep.tile([P, P], F32, name="result%d" % j)
+            nc.scalar.copy(out=result[:], in_=acc[:])
+            nc.sync.dma_start(out=out[:, P * j:P * (j + 1)], in_=result[:])
+
+        linked = [keep.tile([P, SLOTS], F32, name="linked%d" % j, align_bytes=64) for j in range(TILES)]
+        hts = [softplus(0)]
+        turned = [turn_own(0)]
+        neg_max = keep.tile([P, 1], F32, name="neg_max")
+        nc.vector.tensor_reduce(out=neg_max[:], in_=scores[:], axis=AX.X, op=ALU.max, negate=True)
+        prob = keep.tile([P, PACK, P], F32, name="prob", tag="prob", align_bytes=64)
+        row_sum = keep.tile([P, 1], F32, name="row_sum")
+        nc.scalar.activation(out=prob[:], in_=scores[:].rearrange("p (s t) -> p t s", t=PACK), func=ACT.Exp,
+                             bias=neg_max[:], accum_out=row_sum[:])
+        look_up(0, 0, False)
+        look_up(0, 1, False)
+        add_linked(0, "term0")
+        hts.append(softplus(1))
+        turned.append(turn_own(1))
+        look_up(1, 0, False)
+        look_up(1, 1, True)
+        add_linked(1, "term1")
+        for j in range(2, TILES):
+            hts.append(softplus(j))
+            turned.append(turn_own(j))
+            look_up(j, 0, True)
+            look_up(j, 1, True)
+
+        inv_sum = keep.tile([P, 1], F32, name="inv_sum")
+        nc.vector.reciprocal(out=inv_sum[:], in_=row_sum[:])
+        weight = keep.tile([P, PACK, P], F32, name="weight", tag="weight", align_bytes=64)
+        nc.vector.tensor_scalar(out=weight[:], in0=prob[:], scalar1=inv_sum[:], scalar2=None, op0=ALU.mult)
+        w_turned = psum.tile([P, PACK, P], F32, name="w_turned", tag="w_turned")
+        for t in range(PACK):
+            nc.tensor.transpose(w_turned[:, t, :], weight[:, t, :], ident[:])
+        grouped0 = scale_round("hg0", turned[0], vs_col, "hg0")
+        w_grouped = scale_round("wg", w_turned, os_col, "wg")
+        h_q0 = quantize("hq0", grouped0)
+        w_codes, w_scales = quantize("wq", w_grouped)
+        add_linked(2, "prob")
+        read_out(0, *h_q0)
+        read_out(1, *quantize("hq1", scale_round("hg1", turned[1], vs_col, "weight")))
+        add_linked(3, "wg")
+        for j in range(2, TILES):
+            read_out(j, *quantize("hq%d" % j, scale_round("hg%d" % j, turned[j], vs_col, "hg%d" % j)))

@@ -150,8 +150,8 @@ def tile_attend_lrlent_soft_kernel(tc, query, keys_words, keys_scales, tab_words
             else:
                 nc.vector.tensor_copy(out=linked[j][:, cols], in_=picked)
 
-        def turn_own(j):
-            bank = psum.tile([P, PACK, P], F32, name="turned%d" % j, tag="zh%d" % j)
+        def turn_own(j, tag):
+            bank = psum.tile([P, PACK, P], F32, name="turned%d" % j, tag=tag)
             for t in range(PACK):
                 nc.tensor.matmul(bank[:, t, :], lhsT=hts[j][:, t:SLOTS:PACK], rhs=ident[:], start=(t == 0),
                                  stop=False, is_transpose=True)
@@ -159,8 +159,9 @@ def tile_attend_lrlent_soft_kernel(tc, query, keys_words, keys_scales, tab_words
 
         def add_linked(j, tag):
             term = keep.tile([P, PACK, P], F32, name="term%d" % j, tag=tag, align_bytes=64)
-            nc.gpsimd.tensor_scalar(out=term[:], in0=linked[j][:].rearrange("p (s t) -> p t s", t=PACK),
-                                    scalar1=lam_col[:, j:j + 1], scalar2=0.0, op0=ALU.mult, op1=ALU.add)
+            nc.vector.tensor_scalar(out=term[:].rearrange("p t (c i) -> p c t i", i=4),
+                                    in0=linked[j][:].rearrange("p (c i t) -> p c t i", i=4, t=PACK),
+                                    scalar1=lam_col[:, j:j + 1], scalar2=None, op0=ALU.mult)
             for t in range(PACK):
                 nc.tensor.matmul(turned[j][:, t, :], lhsT=term[:, t, :], rhs=ident[:], start=False,
                                  stop=(t == PACK - 1), is_transpose=True)
@@ -172,7 +173,7 @@ def tile_attend_lrlent_soft_kernel(tc, query, keys_words, keys_scales, tab_words
             return grouped
 
         def read_out(j, codes, scales):
-            acc = psum.tile([P, P], F32, name="acc%d" % j, tag="acc%d" % (j % 2))
+            acc = psum.tile([P, P], F32, name="acc%d" % j, tag=("acc0", "acc1", "zh2", "zh3")[j])
             nc.tensor.matmul_mx(out=acc[:], lhsT=w_codes[:].bitcast(FP8X4), lhsT_scale=w_scales[:],
                                 rhs=codes[:].bitcast(FP8X4), rhs_scale=scales[:], start=True, stop=True)
             result = keep.tile([P, P], F32, name="result%d" % j)
@@ -181,7 +182,7 @@ def tile_attend_lrlent_soft_kernel(tc, query, keys_words, keys_scales, tab_words
 
         linked = [keep.tile([P, SLOTS], F32, name="linked%d" % j, align_bytes=64) for j in range(TILES)]
         hts = [softplus(0)]
-        turned = [turn_own(0)]
+        turned = [turn_own(0, "zh0")]
         neg_max = keep.tile([P, 1], F32, name="neg_max")
         nc.vector.tensor_reduce(out=neg_max[:], in_=scores[:], axis=AX.X, op=ALU.max, negate=True)
         prob = keep.tile([P, PACK, P], F32, name="prob", tag="prob", align_bytes=64)
@@ -190,17 +191,14 @@ def tile_attend_lrlent_soft_kernel(tc, query, keys_words, keys_scales, tab_words
                              bias=neg_max[:], accum_out=row_sum[:])
         look_up(0, 0, False)
         look_up(0, 1, False)
-        add_linked(0, "term0")
         hts.append(softplus(1))
-        turned.append(turn_own(1))
-        look_up(1, 0, False)
+        add_linked(0, "term0")
+        turned.append(turn_own(1, "zh1"))
+        look_up(1, 0, True)
         look_up(1, 1, True)
-        add_linked(1, "term1")
-        for j in range(2, TILES):
-            hts.append(softplus(j))
-            turned.append(turn_own(j))
-            look_up(j, 0, True)
-            look_up(j, 1, True)
+        hts.append(softplus(2))
+        look_up(2, 0, True)
+        look_up(2, 1, True)
 
         inv_sum = keep.tile([P, 1], F32, name="inv_sum")
         nc.vector.reciprocal(out=inv_sum[:], in_=row_sum[:])
@@ -210,12 +208,21 @@ def tile_attend_lrlent_soft_kernel(tc, query, keys_words, keys_scales, tab_words
         for t in range(PACK):
             nc.tensor.transpose(w_turned[:, t, :], weight[:, t, :], ident[:])
         grouped0 = scale_round("hg0", turned[0], vs_col, "hg0")
+        hts.append(softplus(3))
+        look_up(3, 0, True)
+        look_up(3, 1, True)
+        add_linked(1, "term1")
+        turned.append(turn_own(2, "zh0"))
         w_grouped = scale_round("wg", w_turned, os_col, "wg")
+        turned.append(turn_own(3, "w_turned"))
         h_q0 = quantize("hq0", grouped0)
         w_codes, w_scales = quantize("wq", w_grouped)
-        add_linked(2, "prob")
         read_out(0, *h_q0)
-        read_out(1, *quantize("hq1", scale_round("hg1", turned[1], vs_col, "weight")))
-        add_linked(3, "wg")
-        for j in range(2, TILES):
-            read_out(j, *quantize("hq%d" % j, scale_round("hg%d" % j, turned[j], vs_col, "hg%d" % j)))
+        grouped1 = scale_round("hg1", turned[1], vs_col, "weight")
+        add_linked(2, "wg")
+        read_out(1, *quantize("hq1", grouped1))
+        add_linked(3, "weight")
+        grouped2 = scale_round("hg2", turned[2], vs_col, "hg2")
+        grouped3 = scale_round("hg3", turned[3], vs_col, "hg3")
+        read_out(2, *quantize("hq2", grouped2))
+        read_out(3, *quantize("hq3", grouped3))

from contextlib import ExitStack

import concourse.mybir as mybir
from concourse.masks import make_identity

F32 = mybir.dt.float32
BF16 = mybir.dt.bfloat16
I32 = mybir.dt.int32
U32 = mybir.dt.uint32
U16 = mybir.dt.uint16
U8 = mybir.dt.uint8
FP8X4 = mybir.dt.float8_e4m3fn_x4
ACT = mybir.ActivationFunctionType
ALU = mybir.AluOpType
AX = mybir.AxisListType

P = 128
PACK = 4
POOL = 2048
SLOTS = 512
HIDDEN = 512
ROWS = 128
TILES = HIDDEN // P
LINEAR_FROM = 40.0

FLOPS = 2 * 512 * ROWS * SLOTS + 2 * 512 * HIDDEN * SLOTS + 2 * SLOTS * ROWS * HIDDEN


def tile_attend_lrlent_soft_kernel(tc, query, keys_words, keys_scales, tab_words, tab_scales, w1, lam,
                                    slot_factor, value_scale, offs3, offs, out):
    nc = tc.nc
    with ExitStack() as ctx:
        keep = ctx.enter_context(tc.tile_pool(name="keep", bufs=1))
        shared = ctx.enter_context(tc.tile_pool(name="shared", bufs=1))
        psum = ctx.enter_context(tc.psum_pool(name="psum", bufs=1))

        def load_scales(name, scales):
            plane = keep.tile([P, POOL], U8, name=name, align_bytes=64)
            nc.gpsimd.memset(plane[:].bitcast(I32), 0)
            for quad in range(4):
                nc.sync.dma_start(out=plane[32 * quad:32 * quad + 4, :].bitcast(I32),
                                  in_=scales[0, 4 * quad:4 * quad + 4, :].bitcast(I32))
            return plane

        def load_scales_repeated(name, scales):
            plane = keep.tile([P, POOL], U8, name=name, align_bytes=64)
            for quad in range(4):
                rows = scales[0, 4 * quad:4 * quad + 4, :].bitcast(I32)
                nc.sync.dma_start(out=plane[32 * quad:32 * quad + 32, :].bitcast(I32),
                                  in_=rows.unsqueeze(0).to_broadcast([8, 4, POOL // 4]))
            return plane

        def load_words(pool_words, words):
            nc.sync.dma_start(out=pool_words[:], in_=words[0].rearrange("p n t -> p (n t)").bitcast(I32))
            return pool_words

        def gather_scales(name, plane, tag):
            picked = keep.tile([P, SLOTS], U8, name=name, tag=tag, align_bytes=64)
            nc.vector.tensor_copy(out=picked[:], in_=plane[:].indirect(tokens[:]))
            return picked

        def gather_words(name, pool_words):
            picked = keep.tile([P, SLOTS], U32, name=name, align_bytes=64)
            nc.vector.tensor_copy(out=picked[:], in_=pool_words[:].bitcast(U32).indirect(tokens[:]))
            return picked

        def quantize(name, grouped):
            codes = keep.tile([P, P], U32, name=name + "_codes", align_bytes=64)
            scales = keep.tile([P, P], U8, name=name + "_scales", align_bytes=64)
            nc.vector.quantize_mx(out=codes[:].bitcast(FP8X4), scales=scales[:],
                                  in_=grouped[:].rearrange("p c t -> p (c t)"))
            return codes, scales

        def weave(name, raw, on_scalar, tag):
            grouped = keep.tile([P, P, PACK], BF16, name=name, tag=tag, align_bytes=64)
            dst = grouped[:].rearrange("p (c i) t -> p c t i", i=4)
            src = raw.rearrange("p t (c i) -> p c t i", i=4)
            if on_scalar:
                nc.scalar.activation(out=dst, in_=src, func=ACT.Copy)
            else:
                nc.vector.tensor_copy(out=dst, in_=src)
            return grouped

        tokens = keep.tile([P, SLOTS // 16], U16, name="tokens")
        nc.sync.dma_start(tokens[:], offs)
        tab_plane = load_scales_repeated("tab_plane", tab_scales)
        tab_pool = load_words(keep.tile([P, POOL], I32, name="tab_pool", align_bytes=64), tab_words)
        w1_rows = w1.rearrange("(p t) r -> p t r", t=PACK)
        w1_raw = []
        for half in range(2):
            raw = keep.tile([P, PACK, 2 * P], F32, name="w1_raw%d" % half, align_bytes=64)
            nc.sync.dma_start(out=raw[:], in_=w1_rows[:, :, 2 * P * half:2 * P * (half + 1)])
            w1_raw.append(raw)
        keys_plane = load_scales("keys_plane", keys_scales)
        query_raw = keep.tile([P, PACK, ROWS], F32, name="query_raw", align_bytes=64)
        nc.sync.dma_start(out=query_raw[:], in_=query.rearrange("(p t) q -> p t q", t=PACK))
        keys_pool = load_words(shared.tile([P, POOL], I32, name="keys_pool", align_bytes=64, offset=0), keys_words)
        links = keep.tile([P, SLOTS // 16], U16, name="links")
        nc.sync.dma_start(links[:], offs3)
        lam_col = keep.tile([P, TILES], F32, name="lam_col")
        with nc.allow_non_contiguous_dma(reason="one factor a partition and tile"):
            nc.sync.dma_start(out=lam_col[:], in_=lam.rearrange("(j p) o -> p (j o)", p=P))
        vs_col = keep.tile([P, PACK], F32, name="vs_col")
        nc.sync.dma_start(out=vs_col[:], in_=value_scale.rearrange("o (p t) -> p (o t)", t=PACK))
        os_col = keep.tile([P, PACK], F32, name="os_col")
        nc.sync.dma_start(out=os_col[:], in_=slot_factor.rearrange("o (p t) -> p (o t)", t=PACK))

        ident = keep.tile([P, P], F32, name="ident", align_bytes=64)
        make_identity(nc, ident[:])

        tab_s = gather_scales("tab_s", tab_plane, "tab_s")
        tab_w = gather_words("tab_w", tab_pool)
        zh = []
        grown = []
        for j in range(TILES):
            raw = w1_raw[j // 2][:, :, P * (j % 2):P * (j % 2 + 1)]
            codes, scales = quantize("w1q%d" % j, weave("w1g%d" % j, raw, j == 1, "w1g%d" % j))
            bank = psum.tile([P, SLOTS], F32, name="zh%d" % j, tag="zh%d" % j)
            nc.tensor.matmul_mx(out=bank[:], lhsT=codes[:].bitcast(FP8X4), lhsT_scale=scales[:],
                                rhs=tab_w[:].bitcast(FP8X4), rhs_scale=tab_s[:], start=True, stop=True)
            e = keep.tile([P, SLOTS], F32, name="grown%d" % j)
            nc.scalar.activation(out=e[:], in_=bank[:], func=ACT.Exp)
            zh.append(bank)
            grown.append(e)

        keys_s = gather_scales("keys_s", keys_plane, "w1g3")
        q_codes, q_scales = quantize("qq", weave("qg", query_raw[:], False, "w1g2"))
        keys_w = gather_words("keys_w", keys_pool)
        scores = psum.tile([P, SLOTS], F32, name="scores", tag="scores")
        nc.tensor.matmul_mx(out=scores[:], lhsT=q_codes[:].bitcast(FP8X4), lhsT_scale=q_scales[:],
                            rhs=keys_w[:].bitcast(FP8X4), rhs_scale=keys_s[:], start=True, stop=True)

        logs = []
        for j in range(TILES):
            lg = keep.tile([P, SLOTS], F32, name="log%d" % j)
            nc.scalar.activation(out=lg[:], in_=grown[j][:], func=ACT.Ln, bias=1.0)
            logs.append(lg)

        def softplus(j):
            ht = shared.tile([P, SLOTS], F32, name="ht%d" % j, align_bytes=64, offset=4 * SLOTS * j)
            nc.vector.scalar_tensor_tensor(out=ht[:], in0=logs[j][:], scalar=LINEAR_FROM, in1=zh[j][:],
                                           op0=ALU.min, op1=ALU.max)
            return ht

        def look_up(j, half, on_scalar):
            cols = slice(256 * half, 256 * (half + 1))
            picked = hts[j][:].indirect(links[:, 16 * half:16 * (half + 1)])
            if on_scalar:
                nc.scalar.activation(out=linked[j][:, cols], in_=picked, func=ACT.Copy)
            else:
                nc.vector.tensor_copy(out=linked[j][:, cols], in_=picked)

        def turn_own(j, tag):
            bank = psum.tile([P, PACK, P], F32, name="turned%d" % j, tag=tag)
            for t in range(PACK):
                nc.tensor.matmul(bank[:, t, :], lhsT=hts[j][:, t:SLOTS:PACK], rhs=ident[:], start=(t == 0),
                                 stop=False, is_transpose=True)
            return bank

        def add_linked(j, tag):
            term = keep.tile([P, PACK, P], F32, name="term%d" % j, tag=tag, align_bytes=64)
            nc.vector.tensor_scalar(out=term[:].rearrange("p t (c i) -> p c t i", i=4),
                                    in0=linked[j][:].rearrange("p (c i t) -> p c t i", i=4, t=PACK),
                                    scalar1=lam_col[:, j:j + 1], scalar2=None, op0=ALU.mult)
            for t in range(PACK):
                nc.tensor.matmul(turned[j][:, t, :], lhsT=term[:, t, :], rhs=ident[:], start=False,
                                 stop=(t == PACK - 1), is_transpose=True)

        def scale_round(name, bank, col, tag):
            grouped = keep.tile([P, P, PACK], BF16, name=name, tag=tag, align_bytes=64)
            nc.vector.tensor_tensor(out=grouped[:], in0=bank[:].rearrange("p t c -> p c t"),
                                    in1=col[:].unsqueeze(1).to_broadcast([P, P, PACK]), op=ALU.mult)
            return grouped

        def read_out(j, codes, scales):
            acc = psum.tile([P, P], F32, name="acc%d" % j, tag=("acc0", "acc1", "zh2", "zh3")[j])
            nc.tensor.matmul_mx(out=acc[:], lhsT=w_codes[:].bitcast(FP8X4), lhsT_scale=w_scales[:],
                                rhs=codes[:].bitcast(FP8X4), rhs_scale=scales[:], start=True, stop=True)
            result = keep.tile([P, P], F32, name="result%d" % j)
            nc.scalar.copy(out=result[:], in_=acc[:])
            nc.sync.dma_start(out=out[:, P * j:P * (j + 1)], in_=result[:])

        linked = [keep.tile([P, SLOTS], F32, name="linked%d" % j, align_bytes=64) for j in range(TILES)]
        hts = [softplus(0)]
        turned = [turn_own(0, "zh0")]
        neg_max = keep.tile([P, 1], F32, name="neg_max")
        nc.vector.tensor_reduce(out=neg_max[:], in_=scores[:], axis=AX.X, op=ALU.max, negate=True)
        prob = keep.tile([P, PACK, P], F32, name="prob", tag="prob", align_bytes=64)
        row_sum = keep.tile([P, 1], F32, name="row_sum")
        nc.scalar.activation(out=prob[:], in_=scores[:].rearrange("p (s t) -> p t s", t=PACK), func=ACT.Exp,
                             bias=neg_max[:], accum_out=row_sum[:])
        look_up(0, 0, False)
        look_up(0, 1, False)
        hts.append(softplus(1))
        add_linked(0, "term0")
        turned.append(turn_own(1, "zh1"))
        look_up(1, 0, True)
        look_up(1, 1, True)
        hts.append(softplus(2))
        look_up(2, 0, True)
        look_up(2, 1, True)

        inv_sum = keep.tile([P, 1], F32, name="inv_sum")
        nc.vector.reciprocal(out=inv_sum[:], in_=row_sum[:])
        weight = keep.tile([P, PACK, P], F32, name="weight", tag="weight", align_bytes=64)
        nc.vector.tensor_scalar(out=weight[:], in0=prob[:], scalar1=inv_sum[:], scalar2=None, op0=ALU.mult)
        w_turned = psum.tile([P, PACK, P], F32, name="w_turned", tag="w_turned")
        for t in range(PACK):
            nc.tensor.transpose(w_turned[:, t, :], weight[:, t, :], ident[:])
        grouped0 = scale_round("hg0", turned[0], vs_col, "hg0")
        hts.append(softplus(3))
        look_up(3, 0, True)
        look_up(3, 1, True)
        add_linked(1, "term1")
        turned.append(turn_own(2, "zh0"))
        w_grouped = scale_round("wg", w_turned, os_col, "wg")
        turned.append(turn_own(3, "w_turned"))
        h_q0 = quantize("hq0", grouped0)
        w_codes, w_scales = quantize("wq", w_grouped)
        read_out(0, *h_q0)
        grouped1 = scale_round("hg1", turned[1], vs_col, "weight")
        add_linked(2, "wg")
        read_out(1, *quantize("hq1", grouped1))
        add_linked(3, "weight")
        grouped2 = scale_round("hg2", turned[2], vs_col, "hg2")
        grouped3 = scale_round("hg3", turned[3], vs_col, "hg3")
        read_out(2, *quantize("hq2", grouped2))
        read_out(3, *quantize("hq3", grouped3))
